import numpy as np, ml_dtypes
CORES = [4,20,60,84,92,100,116]
N = 7
import mx_ref
NC, KT, G, ROOT = 128, 1, 2, 5
C = np.float32(0.041)
BF = ml_dtypes.bfloat16
def cut(t, i, w=512):
    return t[:, w * i:w * i + w]
def tile(rs):
    return np.stack(rs, axis=2).reshape(128, -1).astype(BF)
def layer(w, X):
    out = []
    for i in range(G):
        for t in range(len(X)):
            p = mx_ref.matmul(mx_ref.quantize(cut(w, len(X) * i + t)), X[t])
            z = p if t == 0 else z + p
        out.append(z)
    return out
def act(Z):
    return [np.maximum(s * z, 0) * C for z in Z for s in (1, -1)]
def setup_inputs(rng):
    def f(*shape):
        return mx_ref.flush((rng.standard_normal(shape, dtype=np.float32) * np.exp2(rng.integers(-2, 3, shape[:-1] + (1,)))).astype(BF))
    return {"x": f(N, 128, KT * 4 * NC), "w1": f(N, 128, G * KT * 512), "w2": f(N, 128, 512)}
def setup_inputs_blocks(rng):
    d = setup_inputs(rng)
    for k in ("x", "w1", "w2"): d[k] = mx_ref.spread(d[k], rng, 4)
    return d
def setup_inputs_wide(rng):
    d = setup_inputs(rng)
    for k in ("x", "w1", "w2"): d[k] = mx_ref.flush((d[k].astype(np.float32) * np.exp2(rng.integers(-8, 9, (N, 1, 1))).astype(np.float32)).astype(BF))
    return d
def setup_inputs_zeros(rng):
    d = setup_inputs(rng); v = d["x"].reshape(N, 128, -1, 4).copy()
    v[np.broadcast_to((rng.random((N, 1, v.shape[2], 1)) < 0.33), v.shape)] = 0
    d["x"] = v.reshape(d["x"].shape)
    return d
def reference(x, w1, w2):
    h = mx_ref.quantize(tile(act(layer(w1[ROOT], [mx_ref.quantize(cut(x[ROOT], t, 4 * NC)) for t in range(KT)]))))
    y = np.zeros((N, 128, NC), np.float32)
    for r in range(N):
        y[r] = mx_ref.matmul(mx_ref.quantize(w2[r]), h)
    return {"y": y}

@@ -1,0 +1,140 @@
+import numpy as np
+from concourse.bass import DstId, RemoteDMATransfer
+from concourse.mybir import dt, AluOpType, ActivationFunctionType
+
+NC = 128
+C = float(np.float32(0.041))
+OWN = 2
+
+SCRATCH = {
+    "xb": ("sbuf", [128, 4 * NC], "bfloat16"),
+    "w1b": ("sbuf", [128, 1024], "bfloat16"),
+    "w2b": ("sbuf", [128, 512], "bfloat16"),
+    "hb": ("sbuf", [128, 4 * NC], "bfloat16"),
+    "xq": ("sbuf", [128, NC], "float8_e4m3fn_x4"), "xs": ("sbuf", [128, NC], "uint8"),
+    "w1q": ("sbuf", [128, 256], "float8_e4m3fn_x4"), "w1s": ("sbuf", [128, 256], "uint8"),
+    "w2q": ("sbuf", [128, 128], "float8_e4m3fn_x4"), "w2s": ("sbuf", [128, 128], "uint8"),
+    "hq": ("sbuf", [128, NC], "float8_e4m3fn_x4"), "hs": ("sbuf", [128, NC], "uint8"),
+    "z0": ("psum", [128, 512], "float32"),
+    "z1": ("psum", [128, 512], "float32"),
+    "yp": ("psum", [128, 512], "float32"),
+    "yb": ("sbuf", [128, NC], "float32"),
+}
+SEMAPHORES = ["ld_x", "ld_w10", "ld_w11", "ld_w2", "q_x", "q_w10", "q_w11", "q_w2", "mm0", "mm1", "act_v", "act_s",
+              "q_h", "arr", "sent", "mm_y", "cp_y", "st_y"]
+
+
+def lanes(mask):
+    return bin(mask).count("1")
+
+
+def common(topo, src, dests):
+    m = topo.mask(src, dests[0])
+    for d in dests[1:]:
+        m &= topo.mask(src, d)
+    return m
+
+
+def schedule(T, topo):
+    root = T.cores[T.root]
+    ranks = [c for c in T.cores if c != root]
+    near = [c for c in ranks if topo.may_write(root, c)]
+    far = [c for c in ranks if not topo.may_write(root, c)]
+    spare = [c for c in range(topo.CHIPS * topo.CORES_PER_CHIP)
+             if topo.chip(c) == topo.chip(root) and T.rank_of(c) is None]
+    home = [c for c in spare if topo.die(c) == topo.die(root)]
+    away = [c for c in spare if topo.die(c) != topo.die(root)]
+    port = [c for c in home + away if all(topo.may_write(c, d) for d in far)][:2]
+    rest = [c for c in away + home if c not in port]
+    own, lent = near[:OWN], near[OWN:]
+    jobs = [(port[0], "q", far), (port[1], "s", far)]
+    if lent:
+        jobs += [(rest[0], "q", lent), (rest[1], "s", lent)]
+    helpers = [h for h, part, dests in jobs]
+    wide = common(topo, root, helpers)
+    out = common(topo, root, near)
+    feed = (wide & ~out) or wide
+    sends = [(root, part, [h for h, p, dests in jobs if p == part], feed) for part in ("q", "s")]
+    if own:
+        sends += [(root, part, own, out) for part in ("q", "s")]
+    sends += [(h, part, dests, common(topo, h, dests)) for h, part, dests in jobs]
+    return root, sends
+
+
+def rank_program(g, core, T, topo):
+    S = T.sem
+    root, sends = schedule(T, topo)
+    mine = [s for s in sends if s[0] == core]
+    due = sum(lanes(m) for src, part, dests, m in sends if core in dests)
+    rank = T.rank_of(core)
+    if rank is None and not mine:
+        return
+    view = {"q": T.hq[:].bitcast(dt.uint8), "s": T.hs[:]}
+
+    def issue():
+        left = 0
+        for src, part, dests, m in mine:
+            ids = []
+            for d in dests:
+                a = topo.addr(d)
+                ids.append(DstId(rid=a[0], pnc=a[1]))
+            g.remote_dma_fused([RemoteDMATransfer(dst_ids=ids, dma_engine_mask=m, remote_sem=S.arr,
+                                                  srcs=[view[part]], dsts=[view[part]] * len(dests))],
+                               local_sem=S.sent)
+            left += lanes(m)
+        g.wait_ge(S.sent, left)
+
+    if rank is None:
+        g.wait_ge(S.arr, due)
+        issue()
+        return
+
+    v, t, a, sy = g.vector, g.tensor, g.scalar, g.sync
+    if core == root:
+        sy.dma_start(T.xb[:], T.x[:]).then_inc(S.ld_x, 16)
+        a.dma_start(T.w1b[:, 0:512], T.w1[:, 0:512]).then_inc(S.ld_w10, 16)
+        sy.dma_start(T.w1b[:, 512:1024], T.w1[:, 512:1024]).then_inc(S.ld_w11, 16)
+        sy.wait_ge(S.ld_w11, 16)
+        sy.dma_start(T.w2b[:], T.w2[:]).then_inc(S.ld_w2, 16)
+
+        v.wait_ge(S.ld_x, 16)
+        v.quantize_mx(T.xq[:], T.xs[:], T.xb[:]).then_inc(S.q_x, 1)
+        v.wait_ge(S.ld_w10, 16)
+        v.quantize_mx(T.w1q[:, 0:128], T.w1s[:, 0:128], T.w1b[:, 0:512]).then_inc(S.q_w10, 1)
+        v.wait_ge(S.ld_w11, 16)
+        v.quantize_mx(T.w1q[:, 128:256], T.w1s[:, 128:256], T.w1b[:, 512:1024]).then_inc(S.q_w11, 1)
+
+        t.wait_ge(S.q_x, 1)
+        t.wait_ge(S.q_w10, 1)
+        t.matmul_mx(T.z0[:, 0:NC], T.w1q[:, 0:128], T.w1s[:, 0:128], T.xq[:], T.xs[:], True, True).then_inc(S.mm0, 1)
+        t.wait_ge(S.q_w11, 1)
+        t.matmul_mx(T.z1[:, 0:NC], T.w1q[:, 128:256], T.w1s[:, 128:256], T.xq[:], T.xs[:], True, True).then_inc(S.mm1, 1)
+
+        v.wait_ge(S.mm0, 1)
+        v.tensor_scalar(T.hb[:, 0:4 * NC:4], T.z0[:, 0:NC], 0.0, C, AluOpType.max, AluOpType.mult).then_inc(S.act_v, 1)
+        v.tensor_scalar(T.hb[:, 1:4 * NC:4], T.z0[:, 0:NC], -C, 0.0, AluOpType.mult, AluOpType.max).then_inc(S.act_v, 1)
+        a.wait_ge(S.mm1, 1)
+        a.activation(T.hb[:, 2:4 * NC:4], T.z1[:, 0:NC], ActivationFunctionType.Relu, scale=C).then_inc(S.act_s, 1)
+        a.activation(T.hb[:, 3:4 * NC:4], T.z1[:, 0:NC], ActivationFunctionType.Relu, scale=-C).then_inc(S.act_s, 1)
+        v.wait_ge(S.act_v, 2)
+        v.wait_ge(S.act_s, 2)
+        v.quantize_mx(T.hq[:], T.hs[:], T.hb[:]).then_inc(S.q_h, 1)
+        t.wait_ge(S.q_h, 1)
+    else:
+        sy.dma_start(T.w2b[:], T.w2[:]).then_inc(S.ld_w2, 16)
+
+    v.wait_ge(S.ld_w2, 16)
+    v.quantize_mx(T.w2q[:], T.w2s[:], T.w2b[:]).then_inc(S.q_w2, 1)
+    t.wait_ge(S.q_w2, 1)
+    if core != root:
+        t.wait_ge(S.arr, due)
+    t.matmul_mx(T.yp[:, 0:NC], T.w2q[:], T.w2s[:], T.hq[:], T.hs[:], True, True).then_inc(S.mm_y, 1)
+    v.wait_ge(S.mm_y, 1)
+    v.tensor_copy(T.yb[:], T.yp[:, 0:NC]).then_inc(S.cp_y, 1)
+    sy.wait_ge(S.cp_y, 1)
+    sy.dma_start(T.y[:], T.yb[:]).then_inc(S.st_y, 16)
+    sy.wait_ge(S.st_y, 16)
+
+    if core == root:
+        g.wait_ge(S.q_h, 1)
+        issue()

@@ -4,15 +4,13 @@ from concourse.mybir import dt, AluOpType, ActivationFunctionType
 
 NC = 128
 C = float(np.float32(0.041))
-OWN = 2
 
 SCRATCH = {
     "xb": ("sbuf", [128, 4 * NC], "bfloat16"),
     "w1b": ("sbuf", [128, 1024], "bfloat16"),
     "w2b": ("sbuf", [128, 512], "bfloat16"),
     "hb": ("sbuf", [128, 4 * NC], "bfloat16"),
-    "xq": ("sbuf", [128, NC], "float8_e4m3fn_x4"), "xs": ("sbuf", [128, NC], "uint8"),
-    "w1q": ("sbuf", [128, 256], "float8_e4m3fn_x4"), "w1s": ("sbuf", [128, 256], "uint8"),
+    "aq": ("sbuf", [128, 384], "float8_e4m3fn_x4"), "az": ("sbuf", [128, 384], "uint8"),
     "w2q": ("sbuf", [128, 128], "float8_e4m3fn_x4"), "w2s": ("sbuf", [128, 128], "uint8"),
     "hq": ("sbuf", [128, NC], "float8_e4m3fn_x4"), "hs": ("sbuf", [128, NC], "uint8"),
     "z0": ("psum", [128, 512], "float32"),
@@ -21,7 +19,7 @@ SCRATCH = {
     "yb": ("sbuf", [128, NC], "float32"),
 }
 SEMAPHORES = ["ld_x", "ld_w10", "ld_w11", "ld_w2", "q_x", "q_w10", "q_w11", "q_w2", "mm0", "mm1", "act_v", "act_s",
-              "q_h", "arr", "sent", "mm_y", "cp_y", "st_y"]
+              "q_h", "arr", "ar0", "ar1", "ar2", "sent", "mm_y", "cp_y", "st_y"]
 
 
 def lanes(mask):
@@ -46,50 +44,62 @@ def schedule(T, topo):
     away = [c for c in spare if topo.die(c) != topo.die(root)]
     port = [c for c in home + away if all(topo.may_write(c, d) for d in far)][:2]
     rest = [c for c in away + home if c not in port]
-    own, lent = near[:OWN], near[OWN:]
-    jobs = [(port[0], "q", far), (port[1], "s", far)]
-    if lent:
-        jobs += [(rest[0], "q", lent), (rest[1], "s", lent)]
-    helpers = [h for h, part, dests in jobs]
-    wide = common(topo, root, helpers)
+    car = rest[-1]
+    twin, last, lent = near[0], near[1], near[2:]
+    jobs = [(port[0], "hq", far), (port[1], "hs", far), (rest[0], "hq", lent), (rest[1], "hs", lent)]
+    wide = common(topo, root, [h for h, p, d in jobs] + [car])
     out = common(topo, root, near)
-    feed = (wide & ~out) or wide
-    sends = [(root, part, [h for h, p, dests in jobs if p == part], feed) for part in ("q", "s")]
-    if own:
-        sends += [(root, part, own, out) for part in ("q", "s")]
-    sends += [(h, part, dests, common(topo, h, dests)) for h, part, dests in jobs]
-    return root, sends
+    stay = (wide & ~out) or wide
+    sends = [(root, "xs", [car], stay, "ar0", "q_x"),
+             (root, "hq", [h for h, p, d in jobs if p == "hq"], stay, "arr", "q_h"),
+             (root, "hs", [h for h, p, d in jobs if p == "hs"], stay, "arr", None),
+             (root, "xq", [car], stay, "ar1", None),
+             (root, "wq", [twin], out, "arr", None),
+             (root, "ws", [twin], out, "arr", None),
+             (root, "hq", [car], stay, "ar2", None),
+             (root, "hs", [car], stay, "ar2", None)]
+    sends += [(h, part, dests, common(topo, h, dests), "arr", "arr") for h, part, dests in jobs]
+    sends += [(car, "xs", [twin], topo.mask(car, twin), "arr", "ar0"),
+              (car, "xq", [twin], topo.mask(car, twin), "arr", "ar1"),
+              (car, "hq", [last], topo.mask(car, last), "arr", "ar2"),
+              (car, "hs", [last], topo.mask(car, last), "arr", None)]
+    return root, twin, sends
 
 
 def rank_program(g, core, T, topo):
     S = T.sem
-    root, sends = schedule(T, topo)
+    root, twin, sends = schedule(T, topo)
     mine = [s for s in sends if s[0] == core]
-    due = sum(lanes(m) for src, part, dests, m in sends if core in dests)
+    due = {}
+    for src, part, dests, m, sem, gate in sends:
+        if core in dests:
+            due[sem] = due.get(sem, 0) + lanes(m)
     rank = T.rank_of(core)
     if rank is None and not mine:
         return
-    view = {"q": T.hq[:].bitcast(dt.uint8), "s": T.hs[:]}
+    view = {"hq": T.hq[:].bitcast(dt.uint8), "hs": T.hs[:],
+            "xq": T.aq[:, 0:128].bitcast(dt.uint8), "wq": T.aq[:, 128:384].bitcast(dt.uint8),
+            "xs": T.az[:, 0:128], "ws": T.az[:, 128:384]}
 
-    def issue():
-        left = 0
-        for src, part, dests, m in mine:
-            ids = []
-            for d in dests:
-                a = topo.addr(d)
-                ids.append(DstId(rid=a[0], pnc=a[1]))
-            g.remote_dma_fused([RemoteDMATransfer(dst_ids=ids, dma_engine_mask=m, remote_sem=S.arr,
-                                                  srcs=[view[part]], dsts=[view[part]] * len(dests))],
-                               local_sem=S.sent)
-            left += lanes(m)
+    left = 0
+    for src, part, dests, m, sem, gate in mine:
+        if gate is not None:
+            g.wait_ge(S[gate], 1 if core == root else due[gate])
+        ids = []
+        for d in dests:
+            ad = topo.addr(d)
+            ids.append(DstId(rid=ad[0], pnc=ad[1]))
+        g.remote_dma_fused([RemoteDMATransfer(dst_ids=ids, dma_engine_mask=m, remote_sem=S[sem],
+                                              srcs=[view[part]], dsts=[view[part]] * len(dests))],
+                           local_sem=S.sent)
+        left += lanes(m)
+    if mine:
         g.wait_ge(S.sent, left)
-
     if rank is None:
-        g.wait_ge(S.arr, due)
-        issue()
         return
 
     v, t, a, sy = g.vector, g.tensor, g.scalar, g.sync
+    xq, xs = T.aq[:, 0:128], T.az[:, 0:128]
     if core == root:
         sy.dma_start(T.xb[:], T.x[:]).then_inc(S.ld_x, 16)
         a.dma_start(T.w1b[:, 0:512], T.w1[:, 0:512]).then_inc(S.ld_w10, 16)
@@ -98,17 +108,26 @@ def rank_program(g, core, T, topo):
         sy.dma_start(T.w2b[:], T.w2[:]).then_inc(S.ld_w2, 16)
 
         v.wait_ge(S.ld_x, 16)
-        v.quantize_mx(T.xq[:], T.xs[:], T.xb[:]).then_inc(S.q_x, 1)
+        v.quantize_mx(xq, xs, T.xb[:]).then_inc(S.q_x, 1)
         v.wait_ge(S.ld_w10, 16)
-        v.quantize_mx(T.w1q[:, 0:128], T.w1s[:, 0:128], T.w1b[:, 0:512]).then_inc(S.q_w10, 1)
+        v.quantize_mx(T.aq[:, 128:256], T.az[:, 128:256], T.w1b[:, 0:512]).then_inc(S.q_w10, 1)
         v.wait_ge(S.ld_w11, 16)
-        v.quantize_mx(T.w1q[:, 128:256], T.w1s[:, 128:256], T.w1b[:, 512:1024]).then_inc(S.q_w11, 1)
+        v.quantize_mx(T.aq[:, 256:384], T.az[:, 256:384], T.w1b[:, 512:1024]).then_inc(S.q_w11, 1)
+    else:
+        sy.dma_start(T.w2b[:], T.w2[:]).then_inc(S.ld_w2, 16)
+        v.wait_ge(S.ld_w2, 16)
+        v.quantize_mx(T.w2q[:], T.w2s[:], T.w2b[:]).then_inc(S.q_w2, 1)
 
-        t.wait_ge(S.q_x, 1)
-        t.wait_ge(S.q_w10, 1)
-        t.matmul_mx(T.z0[:, 0:NC], T.w1q[:, 0:128], T.w1s[:, 0:128], T.xq[:], T.xs[:], True, True).then_inc(S.mm0, 1)
-        t.wait_ge(S.q_w11, 1)
-        t.matmul_mx(T.z1[:, 0:NC], T.w1q[:, 128:256], T.w1s[:, 128:256], T.xq[:], T.xs[:], True, True).then_inc(S.mm1, 1)
+    if core != root:
+        t.wait_ge(S.arr, due["arr"])
+    if core == root or core == twin:
+        if core == root:
+            t.wait_ge(S.q_x, 1)
+            t.wait_ge(S.q_w10, 1)
+        t.matmul_mx(T.z0[:, 0:NC], T.aq[:, 128:256], T.az[:, 128:256], xq, xs, True, True).then_inc(S.mm0, 1)
+        if core == root:
+            t.wait_ge(S.q_w11, 1)
+        t.matmul_mx(T.z1[:, 0:NC], T.aq[:, 256:384], T.az[:, 256:384], xq, xs, True, True).then_inc(S.mm1, 1)
 
         v.wait_ge(S.mm0, 1)
         v.tensor_scalar(T.hb[:, 0:4 * NC:4], T.z0[:, 0:NC], 0.0, C, AluOpType.max, AluOpType.mult).then_inc(S.act_v, 1)
@@ -120,21 +139,14 @@ def rank_program(g, core, T, topo):
         v.wait_ge(S.act_s, 2)
         v.quantize_mx(T.hq[:], T.hs[:], T.hb[:]).then_inc(S.q_h, 1)
         t.wait_ge(S.q_h, 1)
-    else:
-        sy.dma_start(T.w2b[:], T.w2[:]).then_inc(S.ld_w2, 16)
 
-    v.wait_ge(S.ld_w2, 16)
-    v.quantize_mx(T.w2q[:], T.w2s[:], T.w2b[:]).then_inc(S.q_w2, 1)
+    if core == root:
+        v.wait_ge(S.ld_w2, 16)
+        v.quantize_mx(T.w2q[:], T.w2s[:], T.w2b[:]).then_inc(S.q_w2, 1)
     t.wait_ge(S.q_w2, 1)
-    if core != root:
-        t.wait_ge(S.arr, due)
     t.matmul_mx(T.yp[:, 0:NC], T.w2q[:], T.w2s[:], T.hq[:], T.hs[:], True, True).then_inc(S.mm_y, 1)
     v.wait_ge(S.mm_y, 1)
     v.tensor_copy(T.yb[:], T.yp[:, 0:NC]).then_inc(S.cp_y, 1)
     sy.wait_ge(S.cp_y, 1)
     sy.dma_start(T.y[:], T.yb[:]).then_inc(S.st_y, 16)
     sy.wait_ge(S.st_y, 16)
-
-    if core == root:
-        g.wait_ge(S.q_h, 1)
-        issue()

@@ -3,6 +3,7 @@ from concourse.bass import DstId, RemoteDMATransfer
 from concourse.mybir import dt, AluOpType, ActivationFunctionType
 
 NC = 128
+QC = NC // 4
 C = float(np.float32(0.041))
 
 SCRATCH = {
@@ -19,11 +20,17 @@ SCRATCH = {
     "yb": ("sbuf", [128, NC], "float32"),
 }
 SEMAPHORES = ["ld_x", "ld_w10", "ld_w11", "ld_w2", "q_x", "q_w10", "q_w11", "q_w2", "mm0", "mm1", "act_v", "act_s",
-              "q_h", "arr", "ar0", "ar1", "ar2", "sent", "mm_y", "cp_y", "st_y"]
+              "q_h", "arr", "ar0", "ar1", "sent", "mm_y", "cp_y", "st_y"]
 
 
 def lanes(mask):
     return bin(mask).count("1")
+
+
+def halves(mask):
+    bits = [b for b in range(mask.bit_length()) if mask >> b & 1]
+    k = len(bits) // 2
+    return sum(1 << b for b in bits[:k]), sum(1 << b for b in bits[k:])
 
 
 def common(topo, src, dests):
@@ -44,55 +51,59 @@ def schedule(T, topo):
     away = [c for c in spare if topo.die(c) != topo.die(root)]
     port = [c for c in home + away if all(topo.may_write(c, d) for d in far)][:2]
     rest = [c for c in away + home if c not in port]
-    car = rest[-1]
-    twin, last, lent = near[0], near[1], near[2:]
-    jobs = [(port[0], "hq", far), (port[1], "hs", far), (rest[0], "hq", lent), (rest[1], "hs", lent)]
-    wide = common(topo, root, [h for h, p, d in jobs] + [car])
+    twin, own, lent = near[0], near[1], near[2:]
+    jobs = [(port[0], "x0", "hq", far), (rest[0], "x1", "hq", lent),
+            (port[1], "x2", "hs", far), (rest[1], "x3", "hs", lent)]
+    wide = common(topo, root, [j[0] for j in jobs])
     out = common(topo, root, near)
     stay = (wide & ~out) or wide
-    sends = [(root, "xs", [car], stay, "ar0", "q_x"),
-             (root, "hq", [h for h, p, d in jobs if p == "hq"], stay, "arr", "q_h"),
-             (root, "hs", [h for h, p, d in jobs if p == "hs"], stay, "arr", None),
-             (root, "xq", [car], stay, "ar1", None),
-             (root, "wq", [twin], out, "arr", None),
-             (root, "ws", [twin], out, "arr", None),
-             (root, "hq", [car], stay, "ar2", None),
-             (root, "hs", [car], stay, "ar2", None)]
-    sends += [(h, part, dests, common(topo, h, dests), "arr", "arr") for h, part, dests in jobs]
-    sends += [(car, "xs", [twin], topo.mask(car, twin), "arr", "ar0"),
-              (car, "xq", [twin], topo.mask(car, twin), "arr", "ar1"),
-              (car, "hq", [last], topo.mask(car, last), "arr", "ar2"),
-              (car, "hs", [last], topo.mask(car, last), "arr", None)]
-    return root, twin, sends
+    lo, hi = halves(stay)
+    calls = [(root, ["q_x"], [(jobs[0][1], [jobs[0][0]], lo, "ar0"), (jobs[1][1], [jobs[1][0]], hi, "ar0")]),
+             (root, [], [(jobs[2][1], [jobs[2][0]], lo, "ar0"), (jobs[3][1], [jobs[3][0]], hi, "ar0")]),
+             (root, [], [("xs", [twin], out, "arr")]),
+             (root, ["q_w10", "q_w11"], [("wq", [twin], out, "arr")]),
+             (root, ["q_h"], [("hq", [j[0] for j in jobs if j[2] == "hq"], stay, "ar1")]),
+             (root, [], [("hs", [j[0] for j in jobs if j[2] == "hs"], stay, "ar1")]),
+             (root, [], [("ws", [twin], out, "arr")]),
+             (root, [], [("hq", [own], out, "arr")]),
+             (root, [], [("hs", [own], out, "arr")])]
+    for h, early, late, dests in jobs:
+        calls.append((h, ["ar0"], [(early, [twin], topo.mask(h, twin), "arr")]))
+        calls.append((h, ["ar1"], [(late, dests, common(topo, h, dests), "arr")]))
+    return root, twin, calls
 
 
 def rank_program(g, core, T, topo):
     S = T.sem
-    root, twin, sends = schedule(T, topo)
-    mine = [s for s in sends if s[0] == core]
+    root, twin, calls = schedule(T, topo)
+    mine = [c for c in calls if c[0] == core]
     due = {}
-    for src, part, dests, m, sem, gate in sends:
-        if core in dests:
-            due[sem] = due.get(sem, 0) + lanes(m)
+    for src, gates, transfers in calls:
+        for part, dests, m, sem in transfers:
+            if core in dests:
+                due[sem] = due.get(sem, 0) + lanes(m)
     rank = T.rank_of(core)
     if rank is None and not mine:
         return
     view = {"hq": T.hq[:].bitcast(dt.uint8), "hs": T.hs[:],
-            "xq": T.aq[:, 0:128].bitcast(dt.uint8), "wq": T.aq[:, 128:384].bitcast(dt.uint8),
-            "xs": T.az[:, 0:128], "ws": T.az[:, 128:384]}
+            "wq": T.aq[:, 128:384].bitcast(dt.uint8), "xs": T.az[:, 0:128], "ws": T.az[:, 128:384]}
+    for k in range(4):
+        view["x%d" % k] = T.aq[:, QC * k:QC * k + QC].bitcast(dt.uint8)
 
     left = 0
-    for src, part, dests, m, sem, gate in mine:
-        if gate is not None:
+    for src, gates, transfers in mine:
+        for gate in gates:
             g.wait_ge(S[gate], 1 if core == root else due[gate])
-        ids = []
-        for d in dests:
-            ad = topo.addr(d)
-            ids.append(DstId(rid=ad[0], pnc=ad[1]))
-        g.remote_dma_fused([RemoteDMATransfer(dst_ids=ids, dma_engine_mask=m, remote_sem=S[sem],
-                                              srcs=[view[part]], dsts=[view[part]] * len(dests))],
-                           local_sem=S.sent)
-        left += lanes(m)
+        trs = []
+        for part, dests, m, sem in transfers:
+            ids = []
+            for d in dests:
+                ad = topo.addr(d)
+                ids.append(DstId(rid=ad[0], pnc=ad[1]))
+            trs.append(RemoteDMATransfer(dst_ids=ids, dma_engine_mask=m, remote_sem=S[sem],
+                                         srcs=[view[part]], dsts=[view[part]] * len(dests)))
+            left += lanes(m)
+        g.remote_dma_fused(trs, local_sem=S.sent)
     if mine:
         g.wait_ge(S.sent, left)
     if rank is None:
@@ -129,12 +140,12 @@ def rank_program(g, core, T, topo):
             t.wait_ge(S.q_w11, 1)
         t.matmul_mx(T.z1[:, 0:NC], T.aq[:, 256:384], T.az[:, 256:384], xq, xs, True, True).then_inc(S.mm1, 1)
 
-        v.wait_ge(S.mm0, 1)
-        v.tensor_scalar(T.hb[:, 0:4 * NC:4], T.z0[:, 0:NC], 0.0, C, AluOpType.max, AluOpType.mult).then_inc(S.act_v, 1)
-        v.tensor_scalar(T.hb[:, 1:4 * NC:4], T.z0[:, 0:NC], -C, 0.0, AluOpType.mult, AluOpType.max).then_inc(S.act_v, 1)
-        a.wait_ge(S.mm1, 1)
-        a.activation(T.hb[:, 2:4 * NC:4], T.z1[:, 0:NC], ActivationFunctionType.Relu, scale=C).then_inc(S.act_s, 1)
-        a.activation(T.hb[:, 3:4 * NC:4], T.z1[:, 0:NC], ActivationFunctionType.Relu, scale=-C).then_inc(S.act_s, 1)
+        a.wait_ge(S.mm0, 1)
+        a.activation(T.hb[:, 0:4 * NC:4], T.z0[:, 0:NC], ActivationFunctionType.Relu, scale=C).then_inc(S.act_s, 1)
+        a.activation(T.hb[:, 1:4 * NC:4], T.z0[:, 0:NC], ActivationFunctionType.Relu, scale=-C).then_inc(S.act_s, 1)
+        v.wait_ge(S.mm1, 1)
+        v.tensor_scalar(T.hb[:, 2:4 * NC:4], T.z1[:, 0:NC], 0.0, C, AluOpType.max, AluOpType.mult).then_inc(S.act_v, 1)
+        v.tensor_scalar(T.hb[:, 3:4 * NC:4], T.z1[:, 0:NC], -C, 0.0, AluOpType.mult, AluOpType.max).then_inc(S.act_v, 1)
         v.wait_ge(S.act_v, 2)
         v.wait_ge(S.act_s, 2)
         v.quantize_mx(T.hq[:], T.hs[:], T.hb[:]).then_inc(S.q_h, 1)

import numpy as np
from concourse.bass import DstId, RemoteDMATransfer
from concourse.mybir import dt, AluOpType, ActivationFunctionType

NC = 128
QC = NC // 4
C = float(np.float32(0.041))

SCRATCH = {
    "xb": ("sbuf", [128, 4 * NC], "bfloat16"),
    "w1b": ("sbuf", [128, 1024], "bfloat16"),
    "w2b": ("sbuf", [128, 512], "bfloat16"),
    "hb": ("sbuf", [128, 4 * NC], "bfloat16"),
    "aq": ("sbuf", [128, 384], "float8_e4m3fn_x4"), "az": ("sbuf", [128, 384], "uint8"),
    "w2q": ("sbuf", [128, 128], "float8_e4m3fn_x4"), "w2s": ("sbuf", [128, 128], "uint8"),
    "hq": ("sbuf", [128, NC], "float8_e4m3fn_x4"), "hs": ("sbuf", [128, NC], "uint8"),
    "z0": ("psum", [128, 512], "float32"),
    "z1": ("psum", [128, 512], "float32"),
    "yp": ("psum", [128, 512], "float32"),
    "yb": ("sbuf", [128, NC], "float32"),
}
SEMAPHORES = ["ld_x", "ld_w10", "ld_w11", "ld_w2", "q_x", "q_w10", "q_w11", "q_w2", "mm0", "mm1", "act_v", "act_s",
              "q_h", "arr", "ar0", "ar1", "sent", "mm_y", "cp_y", "st_y"]


def lanes(mask):
    return bin(mask).count("1")


def halves(mask):
    bits = [b for b in range(mask.bit_length()) if mask >> b & 1]
    k = len(bits) // 2
    return sum(1 << b for b in bits[:k]), sum(1 << b for b in bits[k:])


def common(topo, src, dests):
    m = topo.mask(src, dests[0])
    for d in dests[1:]:
        m &= topo.mask(src, d)
    return m


def schedule(T, topo):
    root = T.cores[T.root]
    ranks = [c for c in T.cores if c != root]
    near = [c for c in ranks if topo.may_write(root, c)]
    far = [c for c in ranks if not topo.may_write(root, c)]
    spare = [c for c in range(topo.CHIPS * topo.CORES_PER_CHIP)
             if topo.chip(c) == topo.chip(root) and T.rank_of(c) is None]
    home = [c for c in spare if topo.die(c) == topo.die(root)]
    away = [c for c in spare if topo.die(c) != topo.die(root)]
    port = [c for c in home + away if all(topo.may_write(c, d) for d in far)][:2]
    rest = [c for c in away + home if c not in port]
    twin, own, lent = near[0], near[1], near[2:]
    jobs = [(port[0], "x0", "hq", far), (rest[0], "x1", "hq", lent),
            (port[1], "x2", "hs", far), (rest[1], "x3", "hs", lent)]
    wide = common(topo, root, [j[0] for j in jobs])
    out = common(topo, root, near)
    stay = (wide & ~out) or wide
    lo, hi = halves(stay)
    calls = [(root, ["q_x"], [(jobs[0][1], [jobs[0][0]], lo, "ar0"), (jobs[1][1], [jobs[1][0]], hi, "ar0")]),
             (root, [], [(jobs[2][1], [jobs[2][0]], lo, "ar0"), (jobs[3][1], [jobs[3][0]], hi, "ar0")]),
             (root, [], [("xs", [twin], out, "arr")]),
             (root, ["q_w10", "q_w11"], [("wq", [twin], out, "arr")]),
             (root, ["q_h"], [("hq", [j[0] for j in jobs if j[2] == "hq"], stay, "ar1")]),
             (root, [], [("hs", [j[0] for j in jobs if j[2] == "hs"], stay, "ar1")]),
             (root, [], [("ws", [twin], out, "arr")]),
             (root, [], [("hq", [own], out, "arr")]),
             (root, [], [("hs", [own], out, "arr")])]
    for h, early, late, dests in jobs:
        calls.append((h, ["ar0"], [(early, [twin], topo.mask(h, twin), "arr")]))
        calls.append((h, ["ar1"], [(late, dests, common(topo, h, dests), "arr")]))
    return root, twin, calls


def rank_program(g, core, T, topo):
    S = T.sem
    root, twin, calls = schedule(T, topo)
    mine = [c for c in calls if c[0] == core]
    due = {}
    for src, gates, transfers in calls:
        for part, dests, m, sem in transfers:
            if core in dests:
                due[sem] = due.get(sem, 0) + lanes(m)
    rank = T.rank_of(core)
    if rank is None and not mine:
        return
    view = {"hq": T.hq[:].bitcast(dt.uint8), "hs": T.hs[:],
            "wq": T.aq[:, 128:384].bitcast(dt.uint8), "xs": T.az[:, 0:128], "ws": T.az[:, 128:384]}
    for k in range(4):
        view["x%d" % k] = T.aq[:, QC * k:QC * k + QC].bitcast(dt.uint8)

    left = 0
    for src, gates, transfers in mine:
        for gate in gates:
            g.wait_ge(S[gate], 1 if core == root else due[gate])
        trs = []
        for part, dests, m, sem in transfers:
            ids = []
            for d in dests:
                ad = topo.addr(d)
                ids.append(DstId(rid=ad[0], pnc=ad[1]))
            trs.append(RemoteDMATransfer(dst_ids=ids, dma_engine_mask=m, remote_sem=S[sem],
                                         srcs=[view[part]], dsts=[view[part]] * len(dests)))
            left += lanes(m)
        g.remote_dma_fused(trs, local_sem=S.sent)
    if mine:
        g.wait_ge(S.sent, left)
    if rank is None:
        return

    v, t, a, sy = g.vector, g.tensor, g.scalar, g.sync
    xq, xs = T.aq[:, 0:128], T.az[:, 0:128]
    if core == root:
        sy.dma_start(T.xb[:], T.x[:]).then_inc(S.ld_x, 16)
        a.dma_start(T.w1b[:, 0:512], T.w1[:, 0:512]).then_inc(S.ld_w10, 16)
        sy.dma_start(T.w1b[:, 512:1024], T.w1[:, 512:1024]).then_inc(S.ld_w11, 16)
        sy.wait_ge(S.ld_w11, 16)
        sy.dma_start(T.w2b[:], T.w2[:]).then_inc(S.ld_w2, 16)

        v.wait_ge(S.ld_x, 16)
        v.quantize_mx(xq, xs, T.xb[:]).then_inc(S.q_x, 1)
        v.wait_ge(S.ld_w10, 16)
        v.quantize_mx(T.aq[:, 128:256], T.az[:, 128:256], T.w1b[:, 0:512]).then_inc(S.q_w10, 1)
        v.wait_ge(S.ld_w11, 16)
        v.quantize_mx(T.aq[:, 256:384], T.az[:, 256:384], T.w1b[:, 512:1024]).then_inc(S.q_w11, 1)
    else:
        sy.dma_start(T.w2b[:], T.w2[:]).then_inc(S.ld_w2, 16)
        v.wait_ge(S.ld_w2, 16)
        v.quantize_mx(T.w2q[:], T.w2s[:], T.w2b[:]).then_inc(S.q_w2, 1)

    if core != root:
        t.wait_ge(S.arr, due["arr"])
    if core == root or core == twin:
        if core == root:
            t.wait_ge(S.q_x, 1)
            t.wait_ge(S.q_w10, 1)
        t.matmul_mx(T.z0[:, 0:NC], T.aq[:, 128:256], T.az[:, 128:256], xq, xs, True, True).then_inc(S.mm0, 1)
        if core == root:
            t.wait_ge(S.q_w11, 1)
        t.matmul_mx(T.z1[:, 0:NC], T.aq[:, 256:384], T.az[:, 256:384], xq, xs, True, True).then_inc(S.mm1, 1)

        a.wait_ge(S.mm0, 1)
        a.activation(T.hb[:, 0:4 * NC:4], T.z0[:, 0:NC], ActivationFunctionType.Relu, scale=C).then_inc(S.act_s, 1)
        a.activation(T.hb[:, 1:4 * NC:4], T.z0[:, 0:NC], ActivationFunctionType.Relu, scale=-C).then_inc(S.act_s, 1)
        v.wait_ge(S.mm1, 1)
        v.tensor_scalar(T.hb[:, 2:4 * NC:4], T.z1[:, 0:NC], 0.0, C, AluOpType.max, AluOpType.mult).then_inc(S.act_v, 1)
        v.tensor_scalar(T.hb[:, 3:4 * NC:4], T.z1[:, 0:NC], -C, 0.0, AluOpType.mult, AluOpType.max).then_inc(S.act_v, 1)
        v.wait_ge(S.act_v, 2)
        v.wait_ge(S.act_s, 2)
        v.quantize_mx(T.hq[:], T.hs[:], T.hb[:]).then_inc(S.q_h, 1)
        t.wait_ge(S.q_h, 1)

    if core == root:
        v.wait_ge(S.ld_w2, 16)
        v.quantize_mx(T.w2q[:], T.w2s[:], T.w2b[:]).then_inc(S.q_w2, 1)
    t.wait_ge(S.q_w2, 1)
    t.matmul_mx(T.yp[:, 0:NC], T.w2q[:], T.w2s[:], T.hq[:], T.hs[:], True, True).then_inc(S.mm_y, 1)
    v.wait_ge(S.mm_y, 1)
    v.tensor_copy(T.yb[:], T.yp[:, 0:NC]).then_inc(S.cp_y, 1)
    sy.wait_ge(S.cp_y, 1)
    sy.dma_start(T.y[:], T.yb[:]).then_inc(S.st_y, 16)
    sy.wait_ge(S.st_y, 16)
